import numpy as np
import ml_dtypes


def mxq(x, axis, fmt="e4m3"):
    dtype, down = {"e4m3": (ml_dtypes.float8_e4m3fn, 7), "e5m2": (ml_dtypes.float8_e5m2, 14)}[fmt]
    v = np.moveaxis(np.asarray(x, np.float32).astype(ml_dtypes.bfloat16).astype(np.float64), axis, -1)
    blocks = v.reshape(v.shape[:-1] + (-1, 32))
    amax = np.abs(blocks).max(-1, keepdims=True)
    byte = np.maximum(np.where(amax > 0, np.frexp(amax)[1] - 1 + 127, 0) - down, 1)
    scale = np.exp2(byte - 127.0)
    codes = (blocks / scale).astype(np.float32).astype(dtype).astype(np.float64)
    return np.moveaxis((codes * scale).reshape(v.shape), -1, axis)


WIDE = False


def mx_kscale(k):
    if not WIDE:
        return np.ones(k)
    levels = np.array([10, -10, 5, -5, 0])
    if k % 512:
        return np.exp2(np.random.permutation(np.resize(levels, k // 32))).repeat(32)
    a = np.empty((k // 512, 16))
    for p in range(k // 512):
        a[p, :8] = np.random.permutation(np.resize(levels, 8))
        for g in range(8):
            far = levels[np.abs(levels - a[p, g]) >= 10]
            a[p, g + 8] = far[np.random.randint(len(far))]
    return np.exp2(a.ravel()).repeat(32)


def f64(x):
    return np.asarray(x).astype(np.float64)


def striped(idx):
    return np.tile(idx.reshape(-1, 16).T, (8, 1)).astype(np.uint16)


def unstriped(offs):
    return offs[:16].T.reshape(-1).astype(np.int64)


def pack_weight(w):
    k, n = w.shape
    w = f64(np.asarray(w, np.float32).astype(ml_dtypes.bfloat16)).reshape(k // 32, 32, n)
    amax = np.abs(w).max(1)
    byte = np.clip(np.where(amax > 0, np.frexp(amax)[1] - 1 + 127 - 7, 1), 1, 254)
    scaled = (w * np.exp2(127.0 - byte)[:, None, :]).reshape(k, n).astype(np.float32)
    words = np.ascontiguousarray(scaled.reshape(k // 512, 128, 4, n).transpose(0, 1, 3, 2)).astype(ml_dtypes.float8_e4m3fn).view(np.uint8)
    return words, np.ascontiguousarray(byte.astype(np.uint8).reshape(k // 512, 16, n))


def unpack_weight(words, scales):
    g, p, n, _ = words.shape
    vals = np.ascontiguousarray(words).view(ml_dtypes.float8_e4m3fn).astype(np.float64) * np.repeat(np.exp2(scales.astype(np.float64) - 127.0), 8, axis=1)[..., None]
    return vals.transpose(0, 1, 3, 2).reshape(g * 512, n)


def relu(v):
    return np.maximum(v, 0.0)


K, T, S, N, H = 1024, 2048, 512, 128, 512


def setup_inputs():
    n = np.random.standard_normal
    s = mx_kscale(K)[:, None]
    u = mx_kscale(H)
    packed_xT = pack_weight(n((K, T)) * s)
    return {
        "x_words": packed_xT[0],
        "x_scales": packed_xT[1],
        "w1": (n((K, H)) / np.sqrt(K) / s).astype(np.float32),
        "w2": (n((K, H)) / np.sqrt(K) / s).astype(np.float32),
        "load": (np.random.uniform(0.5, 1.5, (H, S))).astype(np.float32),
        "unit": (np.random.uniform(0.6, 1.4, (H, 1)) * u[:, None]).astype(np.float32),
        "w3": (n((H, N)) / np.sqrt(H) / u[:, None]).astype(np.float32),
        "offs": striped(np.random.permutation(T)[:S]),
        "nxt": striped(np.random.permutation(S)),
    }


def reference(x_words, x_scales, w1, w2, load, unit, w3, offs, nxt):
    xq = unpack_weight(x_words, x_scales)[:, unstriped(offs)]
    y = mxq(f64(w1), 0, "e4m3").T @ xq
    tr = mxq(f64(w2), 0, "e4m3").T @ xq
    speed = np.exp(0.8 * np.tanh(tr))
    dwell = (np.log(np.exp(y) + 1.0)) / (speed + 0.3)
    dnx = dwell[:, unstriped(nxt)]
    jam = relu(dnx - dwell)
    flow = f64(load) / (dwell + jam + 0.5)
    hid = f64(unit) * (flow - (0.4 * jam))
    return mxq(f64(w3), 0, "e4m3").T @ mxq(hid, 0, "e4m3")

@@ -1,0 +1,258 @@
+import math
+from contextlib import ExitStack
+
+import concourse.mybir as mybir
+
+K, T, S, N, H = 1024, 2048, 512, 128, 512
+FLOPS = 2 * K * H * S * 2 + 2 * H * N * S
+
+F32 = mybir.dt.float32
+BF16 = mybir.dt.bfloat16
+I32 = mybir.dt.int32
+U32 = mybir.dt.uint32
+U16 = mybir.dt.uint16
+U8 = mybir.dt.uint8
+FP8X4 = mybir.dt.float8_e4m3fn_x4
+ALU = mybir.AluOpType
+ACT = mybir.ActivationFunctionType
+
+P = 128
+PACK = 4
+K_PASS = P * PACK
+PASSES = K // K_PASS
+TINY = 2.0**-40
+HALF = S // 2
+
+
+def tile_picked_yetasc_flow_p_kernel(
+    tc, x_words, x_scales, w1, w2, load, unit, w3, offs, nxt, out
+):
+    nc = tc.nc
+    with ExitStack() as ctx:
+        held = ctx.enter_context(tc.tile_pool(name="held", bufs=1))
+        psum = ctx.enter_context(tc.psum_pool(name="psum", bufs=1))
+
+        def sb(name, shape, dtype):
+            return held.tile(shape, dtype, name=name, align_bytes=64)
+
+        offs_sb = held.tile([P, S // 16], U16, name="offs_sb")
+        nxt_sb = held.tile([P, S // 16], U16, name="nxt_sb")
+
+        scale_table = sb("scale_table", [P, T], U8)
+        nc.vector.memset(scale_table[:].bitcast(I32), 0)
+
+        def weight_rows(w, o):
+            return w[o * K_PASS : (o + 1) * K_PASS, :].rearrange("(p j) c -> p j c", j=PACK)
+
+        w2_raw = [sb("w2_raw%d" % o, [P, PACK, H], F32) for o in range(PASSES)]
+        word_table = [sb("word_table%d" % o, [P, T], U32) for o in range(PASSES)]
+        w1_raw0 = sb("w1_raw0", [P, PACK, H], F32)
+        w1_raw1 = [sb("w1_raw1%d" % h, [P, PACK, H // 2], F32) for h in range(2)]
+        w3_raw = sb("w3_raw", [P, PACK, N], F32)
+        unit_sb = sb("unit_sb", [P, PACK], F32)
+        load_sb = sb("load_sb", [P, PACK * S], F32)
+
+        nc.sync.dma_start(w2_raw[0][:], weight_rows(w2, 0))
+        for q in range(4):
+            nc.sync.dma_start(
+                scale_table[32 * q : 32 * q + 8, :].bitcast(I32),
+                x_scales[:, 4 * q : 4 * q + 4, :].bitcast(I32),
+            )
+        nc.sync.dma_start(offs_sb[:], offs)
+        nc.sync.dma_start(w2_raw[1][:], weight_rows(w2, 1))
+        for o in range(PASSES):
+            nc.sync.dma_start(
+                word_table[o][:].bitcast(I32),
+                x_words[o].rearrange("p n t -> p (n t)").bitcast(I32),
+            )
+        nc.sync.dma_start(w1_raw0[:], weight_rows(w1, 0))
+        for h in range(2):
+            nc.sync.dma_start(w1_raw1[h][:], weight_rows(w1, 1)[:, :, h * 256 : (h + 1) * 256])
+        nc.sync.dma_start(w3_raw[:], w3.rearrange("(p t) n -> p t n", t=PACK))
+        nc.sync.dma_start(unit_sb[:], unit.rearrange("(p t) o -> p (t o)", t=PACK))
+        nc.sync.dma_start(nxt_sb[:], nxt)
+        nc.sync.dma_start(load_sb[:], load.rearrange("(p t) j -> p (t j)", t=PACK))
+
+        def deal(copy, grouped, raw, m0, m1):
+            copy(
+                grouped[:].rearrange("p (t m j) -> p m j t", t=PACK, j=PACK)[:, m0:m1],
+                raw[:].rearrange("p j (m t) -> p m j t", t=PACK),
+            )
+
+        def quantize(codes, scales, grouped, c0, c1):
+            nc.vector.quantize_mx(
+                out=codes[:, c0:c1].bitcast(FP8X4),
+                scales=scales[:, c0:c1],
+                in_=grouped[:, PACK * c0 : PACK * c1],
+            )
+
+        names = ("w2", "w1")
+        grouped = {(n, o): sb("%s_bf%d" % (n, o), [P, PACK * H], BF16) for n in names for o in range(PASSES)}
+        codes = {(n, o): sb("%s_codes%d" % (n, o), [P, H], U32) for n in names for o in range(PASSES)}
+        scales = {(n, o): sb("%s_scales%d" % (n, o), [P, H], U8) for n in names for o in range(PASSES)}
+
+        x_scale = sb("x_scale", [P, S], U8)
+        x_codes = [sb("x_codes%d" % o, [P, S], U32) for o in range(PASSES)]
+
+        for o in range(PASSES):
+            deal(nc.scalar.copy, grouped["w2", o], w2_raw[o], 0, P)
+        nc.vector.tensor_copy(x_scale[:], scale_table[:].indirect(offs_sb[:]))
+        for o in range(PASSES):
+            quantize(codes["w2", o], scales["w2", o], grouped["w2", o], 0, H)
+        nc.vector.tensor_copy(x_codes[0][:], word_table[0][:].indirect(offs_sb[:]))
+        for h in range(2):
+            nc.vector.tensor_copy(
+                x_codes[1][:, h * HALF : (h + 1) * HALF],
+                word_table[1][:].indirect(offs_sb[:, h * HALF // 16 : (h + 1) * HALF // 16]),
+            )
+
+        def product(acc, name, o, t, j0, j1, start, stop):
+            cols = slice(t * P, (t + 1) * P)
+            nc.tensor.matmul_mx(
+                out=acc,
+                lhsT=codes[name, o][:, cols].bitcast(FP8X4),
+                lhsT_scale=scales[name, o][:, cols],
+                rhs=x_codes[o][:, j0:j1].bitcast(FP8X4),
+                rhs_scale=x_scale[4 * o : P, j0:j1],
+                start=start,
+                stop=stop,
+            )
+
+        tr_bank = {
+            (h, u): psum.tile([P, 2, HALF], F32, name="tr%d%d" % (h, u), tag="a%d" % (2 * h + u))
+            for h in range(2)
+            for u in range(2)
+        }
+        y_bank = [psum.tile([P, S], F32, name="y%d" % t, tag="b%d" % t) for t in range(PACK)]
+        for o in range(PASSES):
+            for h in range(2):
+                for t in range(PACK):
+                    u, e = divmod(t, 2)
+                    first, last = (o, e) == (0, 0), (o, e) == (PASSES - 1, 1)
+                    product(tr_bank[h, u][:, e, :], "w2", o, t, h * HALF, (h + 1) * HALF, first, last)
+
+        def cut(tile, h, u):
+            return tile[:].rearrange("p (t j) -> p t j", t=PACK)[:, 2 * u : 2 * u + 2, h * HALF : (h + 1) * HALF]
+
+        def part(tile, t):
+            return tile[:, t * S : (t + 1) * S]
+
+        half_tanh = sb("half_tanh", [P, PACK * S], F32)
+        slow = sb("slow", [P, PACK * S], F32)
+        for h in range(2):
+            for u in range(2):
+                nc.scalar.activation(cut(half_tanh, h, u), tr_bank[h, u][:], ACT.Sigmoid, scale=2.0)
+        nc.scalar.activation(slow[:], half_tanh[:], ACT.Sigmoid, scale=-1.6, bias=0.8 + math.log(0.3))
+
+        deal(nc.vector.tensor_copy, grouped["w1", 0], w1_raw0, 0, P)
+        deal(nc.vector.tensor_copy, grouped["w1", 1], w1_raw1[0], 0, P // 2)
+        quantize(codes["w1", 0], scales["w1", 0], grouped["w1", 0], 0, H)
+        deal(nc.vector.tensor_copy, grouped["w1", 1], w1_raw1[1], P // 2, P)
+        for t in range(PACK):
+            quantize(codes["w1", 1], scales["w1", 1], grouped["w1", 1], t * P, (t + 1) * P)
+        for o in range(PASSES):
+            for t in range(PACK):
+                product(y_bank[t][:], "w1", o, t, 0, S, o == 0, o == PASSES - 1)
+
+        w3_bf = sb("w3_bf", [P, PACK * N], BF16)
+        w3_codes = sb("w3_codes", [P, N], U32)
+        w3_scales = sb("w3_scales", [P, N], U8)
+        nc.vector.tensor_copy(
+            w3_bf[:].rearrange("p (c i t) -> p c t i", i=4, t=PACK),
+            w3_raw[:].rearrange("p t (c i) -> p c t i", i=4),
+        )
+        jam_unit = sb("jam_unit", [P, PACK], F32)
+        nc.vector.tensor_scalar(jam_unit[:], unit_sb[:], -0.4, None, ALU.mult)
+        quantize(w3_codes, w3_scales, w3_bf, 0, N)
+        unit_load = sb("unit_load", [P, PACK * S], F32)
+        for t in range(PACK):
+            nc.vector.tensor_scalar(part(unit_load, t), part(load_sb, t), unit_sb[:, t : t + 1], None, ALU.mult)
+
+        tail = sb("tail", [P, PACK * S], F32)
+        log_tail = sb("log_tail", [P, PACK * S], F32)
+        softplus = sb("softplus", [P, PACK * S], F32)
+        dwell = sb("dwell", [P, PACK * S], F32)
+        for t in range(PACK):
+            nc.scalar.activation(part(tail, t), y_bank[t][:], ACT.Sigmoid, scale=-1.0)
+        for t in range(PACK):
+            nc.scalar.activation(part(log_tail, t), part(tail, t), ACT.Ln, bias=TINY)
+
+        def make_softplus(t):
+            nc.vector.scalar_tensor_tensor(
+                part(softplus, t), part(log_tail, t), -1.0, y_bank[t][:], ALU.mult, ALU.max
+            )
+
+        def make_dwell(t):
+            nc.vector.scalar_tensor_tensor(
+                part(dwell, t), part(slow, t), 1.0 / 0.3, part(softplus, t), ALU.mult, ALU.mult
+            )
+
+        make_softplus(0)
+        for t in range(1, PACK):
+            make_softplus(t)
+            make_dwell(t - 1)
+        make_dwell(PACK - 1)
+
+
+        def finish(hid, c0, w, j0, weave, copy_out, bank):
+            hid_bf = sb("hid_bf%d" % j0, [P, PACK * w], BF16)
+            hid_codes = sb("hid_codes%d" % j0, [P, w], U32)
+            hid_scales = sb("hid_scales%d" % j0, [P, w], U8)
+            result = sb("result%d" % j0, [P, w], F32)
+            weave(
+                hid_bf[:].rearrange("p (c i t) -> p c t i", i=4, t=PACK),
+                hid[:, :, c0 : c0 + w].rearrange("p t (c i) -> p c t i", i=4),
+            )
+            quantize(hid_codes, hid_scales, hid_bf, 0, w)
+            acc = psum.tile([P, w], F32, name="acc%d" % j0, tag="a%d" % bank)
+            nc.tensor.matmul_mx(
+                out=acc[:],
+                lhsT=w3_codes[:].bitcast(FP8X4),
+                lhsT_scale=w3_scales[:],
+                rhs=hid_codes[:].bitcast(FP8X4),
+                rhs_scale=hid_scales[:],
+                start=True,
+                stop=True,
+            )
+            copy_out(result[:], acc[:])
+            nc.sync.dma_start(out[:, j0 : j0 + w], result[:])
+
+        for h in range(2):
+            def pair(name, tag):
+                return [
+                    held.tile([P, 2, HALF], F32, name="%s%d%d" % (name, h, u), tag="%s%d" % (tag, u), align_bytes=64)
+                    for u in range(2)
+                ]
+
+            ahead = pair("ahead", "ahead" if h == 0 else "turn")
+            longest = pair("longest", "longest%d" % h)
+            jam = pair("jam", "jam%d" % h)
+            root = pair("root", "turn" if h == 0 else "root")
+            recip = pair("recip", "recip%d" % h)
+            flow = pair("flow", "flow%d" % h)
+            hid = sb("hid%d" % h, [P, PACK, HALF], BF16)
+            for t in range(PACK):
+                nc.scalar.activation(
+                    ahead[t // 2][:, t % 2, :],
+                    part(dwell, t).indirect(nxt_sb[:, h * HALF // 16 : (h + 1) * HALF // 16]),
+                    ACT.Copy,
+                )
+            for u in range(2):
+                nc.vector.tensor_tensor(longest[u][:], ahead[u][:], cut(dwell, h, u), ALU.max)
+            for u in range(2):
+                nc.scalar.activation(root[u][:], longest[u][:], ACT.Abs_reciprocal_sqrt, bias=0.5)
+                nc.scalar.activation(recip[u][:], root[u][:], ACT.Square)
+            for u in range(2):
+                nc.vector.tensor_tensor(jam[u][:], longest[u][:], cut(dwell, h, u), ALU.subtract)
+            for u in range(2):
+                nc.vector.tensor_tensor(flow[u][:], recip[u][:], cut(unit_load, h, u), ALU.mult)
+                for e in range(2):
+                    t = 2 * u + e
+                    nc.vector.scalar_tensor_tensor(
+                        hid[:, t, :], jam[u][:, e, :], jam_unit[:, t : t + 1], flow[u][:, e, :], ALU.mult, ALU.add
+                    )
+            if h == 0:
+                finish(hid, 0, HALF, 0, nc.scalar.copy, nc.scalar.copy, 0)
+            else:
+                finish(hid, 0, HALF // 2, HALF, nc.vector.tensor_copy, nc.vector.tensor_copy, 1)
+                finish(hid, HALF // 2, HALF // 2, HALF + HALF // 2, nc.scalar.copy, nc.scalar.copy, 2)

@@ -20,7 +20,7 @@ P = 128
 PACK = 4
 K_PASS = P * PACK
 PASSES = K // K_PASS
-TINY = 2.0**-40
+KNEE = 16.0
 HALF = S // 2
 
 
@@ -94,9 +94,9 @@ def tile_picked_yetasc_flow_p_kernel(
         x_scale = sb("x_scale", [P, S], U8)
         x_codes = [sb("x_codes%d" % o, [P, S], U32) for o in range(PASSES)]
 
-        for o in range(PASSES):
-            deal(nc.scalar.copy, grouped["w2", o], w2_raw[o], 0, P)
+        deal(nc.scalar.copy, grouped["w2", 0], w2_raw[0], 0, P)
         nc.vector.tensor_copy(x_scale[:], scale_table[:].indirect(offs_sb[:]))
+        deal(nc.vector.tensor_copy, grouped["w2", 1], w2_raw[1], 0, P)
         for o in range(PASSES):
             quantize(codes["w2", o], scales["w2", o], grouped["w2", o], 0, H)
         nc.vector.tensor_copy(x_codes[0][:], word_table[0][:].indirect(offs_sb[:]))
@@ -154,6 +154,23 @@ def tile_picked_yetasc_flow_p_kernel(
             for t in range(PACK):
                 product(y_bank[t][:], "w1", o, t, 0, S, o == 0, o == PASSES - 1)
 
+        tail = sb("tail", [P, PACK * S], F32)
+        floored = sb("floored", [P, PACK * S], F32)
+        log_tail = sb("log_tail", [P, PACK * S], F32)
+        factor = sb("factor", [P, PACK * S], F32)
+        dwell = sb("dwell", [P, PACK * S], F32)
+        for t in range(PACK):
+            nc.scalar.activation(part(tail, t), y_bank[t][:], ACT.Sigmoid, scale=-1.0)
+        for t in range(PACK):
+            nc.vector.scalar_tensor_tensor(part(factor, t), y_bank[t][:], KNEE, part(slow, t), ALU.max, ALU.mult)
+            nc.vector.tensor_scalar(part(floored, t), part(tail, t), math.exp(-KNEE), None, ALU.max)
+        for t in range(PACK):
+            nc.scalar.activation(part(log_tail, t), part(floored, t), ACT.Ln)
+        for t in range(PACK):
+            nc.vector.scalar_tensor_tensor(
+                part(dwell, t), part(log_tail, t), -1.0 / (0.3 * KNEE), part(factor, t), ALU.mult, ALU.mult
+            )
+
         w3_bf = sb("w3_bf", [P, PACK * N], BF16)
         w3_codes = sb("w3_codes", [P, N], U32)
         w3_scales = sb("w3_scales", [P, N], U8)
@@ -164,37 +181,8 @@ def tile_picked_yetasc_flow_p_kernel(
         jam_unit = sb("jam_unit", [P, PACK], F32)
         nc.vector.tensor_scalar(jam_unit[:], unit_sb[:], -0.4, None, ALU.mult)
         quantize(w3_codes, w3_scales, w3_bf, 0, N)
-        unit_load = sb("unit_load", [P, PACK * S], F32)
-        for t in range(PACK):
-            nc.vector.tensor_scalar(part(unit_load, t), part(load_sb, t), unit_sb[:, t : t + 1], None, ALU.mult)
 
-        tail = sb("tail", [P, PACK * S], F32)
-        log_tail = sb("log_tail", [P, PACK * S], F32)
-        softplus = sb("softplus", [P, PACK * S], F32)
-        dwell = sb("dwell", [P, PACK * S], F32)
-        for t in range(PACK):
-            nc.scalar.activation(part(tail, t), y_bank[t][:], ACT.Sigmoid, scale=-1.0)
-        for t in range(PACK):
-            nc.scalar.activation(part(log_tail, t), part(tail, t), ACT.Ln, bias=TINY)
-
-        def make_softplus(t):
-            nc.vector.scalar_tensor_tensor(
-                part(softplus, t), part(log_tail, t), -1.0, y_bank[t][:], ALU.mult, ALU.max
-            )
-
-        def make_dwell(t):
-            nc.vector.scalar_tensor_tensor(
-                part(dwell, t), part(slow, t), 1.0 / 0.3, part(softplus, t), ALU.mult, ALU.mult
-            )
-
-        make_softplus(0)
-        for t in range(1, PACK):
-            make_softplus(t)
-            make_dwell(t - 1)
-        make_dwell(PACK - 1)
-
-
-        def finish(hid, c0, w, j0, weave, copy_out, bank):
+        def finish(hid, c0, w, j0, weave, copy_out, store, bank):
             hid_bf = sb("hid_bf%d" % j0, [P, PACK * w], BF16)
             hid_codes = sb("hid_codes%d" % j0, [P, w], U32)
             hid_scales = sb("hid_scales%d" % j0, [P, w], U8)
@@ -215,28 +203,25 @@ def tile_picked_yetasc_flow_p_kernel(
                 stop=True,
             )
             copy_out(result[:], acc[:])
-            nc.sync.dma_start(out[:, j0 : j0 + w], result[:])
+            store(out[:, j0 : j0 + w], result[:])
 
         for h in range(2):
-            def pair(name, tag):
-                return [
-                    held.tile([P, 2, HALF], F32, name="%s%d%d" % (name, h, u), tag="%s%d" % (tag, u), align_bytes=64)
-                    for u in range(2)
-                ]
+            cols = slice(h * HALF, (h + 1) * HALF)
+            places = nxt_sb[:, h * HALF // 16 : (h + 1) * HALF // 16]
 
-            ahead = pair("ahead", "ahead" if h == 0 else "turn")
-            longest = pair("longest", "longest%d" % h)
-            jam = pair("jam", "jam%d" % h)
-            root = pair("root", "turn" if h == 0 else "root")
-            recip = pair("recip", "recip%d" % h)
-            flow = pair("flow", "flow%d" % h)
+            def pair(name):
+                return [sb("%s%d%d" % (name, h, u), [P, 2, HALF], F32) for u in range(2)]
+
+            ahead, longest, jam, root, recip, flow = [
+                pair(name) for name in ("ahead", "longest", "jam", "root", "recip", "flow")
+            ]
             hid = sb("hid%d" % h, [P, PACK, HALF], BF16)
             for t in range(PACK):
-                nc.scalar.activation(
-                    ahead[t // 2][:, t % 2, :],
-                    part(dwell, t).indirect(nxt_sb[:, h * HALF // 16 : (h + 1) * HALF // 16]),
-                    ACT.Copy,
-                )
+                window = part(dwell, t).indirect(places)
+                if h == 0 and t >= 2:
+                    nc.vector.tensor_copy(ahead[t // 2][:, t % 2, :], window)
+                else:
+                    nc.scalar.activation(ahead[t // 2][:, t % 2, :], window, ACT.Copy)
             for u in range(2):
                 nc.vector.tensor_tensor(longest[u][:], ahead[u][:], cut(dwell, h, u), ALU.max)
             for u in range(2):
@@ -245,14 +230,26 @@ def tile_picked_yetasc_flow_p_kernel(
             for u in range(2):
                 nc.vector.tensor_tensor(jam[u][:], longest[u][:], cut(dwell, h, u), ALU.subtract)
             for u in range(2):
-                nc.vector.tensor_tensor(flow[u][:], recip[u][:], cut(unit_load, h, u), ALU.mult)
-                for e in range(2):
-                    t = 2 * u + e
+                for t in (2 * u, 2 * u + 1):
                     nc.vector.scalar_tensor_tensor(
-                        hid[:, t, :], jam[u][:, e, :], jam_unit[:, t : t + 1], flow[u][:, e, :], ALU.mult, ALU.add
+                        flow[u][:, t % 2, :],
+                        recip[u][:, t % 2, :],
+                        unit_sb[:, t : t + 1],
+                        part(load_sb, t)[:, cols],
+                        ALU.mult,
+                        ALU.mult,
+                    )
+                for t in (2 * u, 2 * u + 1):
+                    nc.vector.scalar_tensor_tensor(
+                        hid[:, t, :],
+                        jam[u][:, t % 2, :],
+                        jam_unit[:, t : t + 1],
+                        flow[u][:, t % 2, :],
+                        ALU.mult,
+                        ALU.add,
                     )
             if h == 0:
-                finish(hid, 0, HALF, 0, nc.scalar.copy, nc.scalar.copy, 0)
+                finish(hid, 0, HALF, 0, nc.scalar.copy, nc.scalar.copy, nc.sync.dma_start, 0)
             else:
-                finish(hid, 0, HALF // 2, HALF, nc.vector.tensor_copy, nc.vector.tensor_copy, 1)
-                finish(hid, HALF // 2, HALF // 2, HALF + HALF // 2, nc.scalar.copy, nc.scalar.copy, 2)
+                finish(hid, 0, HALF // 2, HALF, nc.vector.tensor_copy, nc.vector.tensor_copy, nc.sync.dma_start, 1)
+                finish(hid, HALF // 2, HALF // 2, HALF + HALF // 2, nc.scalar.copy, nc.scalar.copy, nc.scalar.dma_start, 2)

import math
from contextlib import ExitStack

import concourse.mybir as mybir

K, T, S, N, H = 1024, 2048, 512, 128, 512
FLOPS = 2 * K * H * S * 2 + 2 * H * N * S

F32 = mybir.dt.float32
BF16 = mybir.dt.bfloat16
I32 = mybir.dt.int32
U32 = mybir.dt.uint32
U16 = mybir.dt.uint16
U8 = mybir.dt.uint8
FP8X4 = mybir.dt.float8_e4m3fn_x4
ALU = mybir.AluOpType
ACT = mybir.ActivationFunctionType

P = 128
PACK = 4
K_PASS = P * PACK
PASSES = K // K_PASS
KNEE = 16.0
HALF = S // 2


def tile_picked_yetasc_flow_p_kernel(
    tc, x_words, x_scales, w1, w2, load, unit, w3, offs, nxt, out
):
    nc = tc.nc
    with ExitStack() as ctx:
        held = ctx.enter_context(tc.tile_pool(name="held", bufs=1))
        psum = ctx.enter_context(tc.psum_pool(name="psum", bufs=1))

        def sb(name, shape, dtype):
            return held.tile(shape, dtype, name=name, align_bytes=64)

        offs_sb = held.tile([P, S // 16], U16, name="offs_sb")
        nxt_sb = held.tile([P, S // 16], U16, name="nxt_sb")

        scale_table = sb("scale_table", [P, T], U8)
        nc.vector.memset(scale_table[:].bitcast(I32), 0)

        def weight_rows(w, o):
            return w[o * K_PASS : (o + 1) * K_PASS, :].rearrange("(p j) c -> p j c", j=PACK)

        w2_raw = [sb("w2_raw%d" % o, [P, PACK, H], F32) for o in range(PASSES)]
        word_table = [sb("word_table%d" % o, [P, T], U32) for o in range(PASSES)]
        w1_raw0 = sb("w1_raw0", [P, PACK, H], F32)
        w1_raw1 = [sb("w1_raw1%d" % h, [P, PACK, H // 2], F32) for h in range(2)]
        w3_raw = sb("w3_raw", [P, PACK, N], F32)
        unit_sb = sb("unit_sb", [P, PACK], F32)
        load_sb = sb("load_sb", [P, PACK * S], F32)

        nc.sync.dma_start(w2_raw[0][:], weight_rows(w2, 0))
        for q in range(4):
            nc.sync.dma_start(
                scale_table[32 * q : 32 * q + 8, :].bitcast(I32),
                x_scales[:, 4 * q : 4 * q + 4, :].bitcast(I32),
            )
        nc.sync.dma_start(offs_sb[:], offs)
        nc.sync.dma_start(w2_raw[1][:], weight_rows(w2, 1))
        for o in range(PASSES):
            nc.sync.dma_start(
                word_table[o][:].bitcast(I32),
                x_words[o].rearrange("p n t -> p (n t)").bitcast(I32),
            )
        nc.sync.dma_start(w1_raw0[:], weight_rows(w1, 0))
        for h in range(2):
            nc.sync.dma_start(w1_raw1[h][:], weight_rows(w1, 1)[:, :, h * 256 : (h + 1) * 256])
        nc.sync.dma_start(w3_raw[:], w3.rearrange("(p t) n -> p t n", t=PACK))
        nc.sync.dma_start(unit_sb[:], unit.rearrange("(p t) o -> p (t o)", t=PACK))
        nc.sync.dma_start(nxt_sb[:], nxt)
        nc.sync.dma_start(load_sb[:], load.rearrange("(p t) j -> p (t j)", t=PACK))

        def deal(copy, grouped, raw, m0, m1):
            copy(
                grouped[:].rearrange("p (t m j) -> p m j t", t=PACK, j=PACK)[:, m0:m1],
                raw[:].rearrange("p j (m t) -> p m j t", t=PACK),
            )

        def quantize(codes, scales, grouped, c0, c1):
            nc.vector.quantize_mx(
                out=codes[:, c0:c1].bitcast(FP8X4),
                scales=scales[:, c0:c1],
                in_=grouped[:, PACK * c0 : PACK * c1],
            )

        names = ("w2", "w1")
        grouped = {(n, o): sb("%s_bf%d" % (n, o), [P, PACK * H], BF16) for n in names for o in range(PASSES)}
        codes = {(n, o): sb("%s_codes%d" % (n, o), [P, H], U32) for n in names for o in range(PASSES)}
        scales = {(n, o): sb("%s_scales%d" % (n, o), [P, H], U8) for n in names for o in range(PASSES)}

        x_scale = sb("x_scale", [P, S], U8)
        x_codes = [sb("x_codes%d" % o, [P, S], U32) for o in range(PASSES)]

        deal(nc.scalar.copy, grouped["w2", 0], w2_raw[0], 0, P)
        nc.vector.tensor_copy(x_scale[:], scale_table[:].indirect(offs_sb[:]))
        deal(nc.vector.tensor_copy, grouped["w2", 1], w2_raw[1], 0, P)
        for o in range(PASSES):
            quantize(codes["w2", o], scales["w2", o], grouped["w2", o], 0, H)
        nc.vector.tensor_copy(x_codes[0][:], word_table[0][:].indirect(offs_sb[:]))
        for h in range(2):
            nc.vector.tensor_copy(
                x_codes[1][:, h * HALF : (h + 1) * HALF],
                word_table[1][:].indirect(offs_sb[:, h * HALF // 16 : (h + 1) * HALF // 16]),
            )

        def product(acc, name, o, t, j0, j1, start, stop):
            cols = slice(t * P, (t + 1) * P)
            nc.tensor.matmul_mx(
                out=acc,
                lhsT=codes[name, o][:, cols].bitcast(FP8X4),
                lhsT_scale=scales[name, o][:, cols],
                rhs=x_codes[o][:, j0:j1].bitcast(FP8X4),
                rhs_scale=x_scale[4 * o : P, j0:j1],
                start=start,
                stop=stop,
            )

        tr_bank = {
            (h, u): psum.tile([P, 2, HALF], F32, name="tr%d%d" % (h, u), tag="a%d" % (2 * h + u))
            for h in range(2)
            for u in range(2)
        }
        y_bank = [psum.tile([P, S], F32, name="y%d" % t, tag="b%d" % t) for t in range(PACK)]
        for o in range(PASSES):
            for h in range(2):
                for t in range(PACK):
                    u, e = divmod(t, 2)
                    first, last = (o, e) == (0, 0), (o, e) == (PASSES - 1, 1)
                    product(tr_bank[h, u][:, e, :], "w2", o, t, h * HALF, (h + 1) * HALF, first, last)

        def cut(tile, h, u):
            return tile[:].rearrange("p (t j) -> p t j", t=PACK)[:, 2 * u : 2 * u + 2, h * HALF : (h + 1) * HALF]

        def part(tile, t):
            return tile[:, t * S : (t + 1) * S]

        half_tanh = sb("half_tanh", [P, PACK * S], F32)
        slow = sb("slow", [P, PACK * S], F32)
        for h in range(2):
            for u in range(2):
                nc.scalar.activation(cut(half_tanh, h, u), tr_bank[h, u][:], ACT.Sigmoid, scale=2.0)
        nc.scalar.activation(slow[:], half_tanh[:], ACT.Sigmoid, scale=-1.6, bias=0.8 + math.log(0.3))

        deal(nc.vector.tensor_copy, grouped["w1", 0], w1_raw0, 0, P)
        deal(nc.vector.tensor_copy, grouped["w1", 1], w1_raw1[0], 0, P // 2)
        quantize(codes["w1", 0], scales["w1", 0], grouped["w1", 0], 0, H)
        deal(nc.vector.tensor_copy, grouped["w1", 1], w1_raw1[1], P // 2, P)
        for t in range(PACK):
            quantize(codes["w1", 1], scales["w1", 1], grouped["w1", 1], t * P, (t + 1) * P)
        for o in range(PASSES):
            for t in range(PACK):
                product(y_bank[t][:], "w1", o, t, 0, S, o == 0, o == PASSES - 1)

        tail = sb("tail", [P, PACK * S], F32)
        floored = sb("floored", [P, PACK * S], F32)
        log_tail = sb("log_tail", [P, PACK * S], F32)
        factor = sb("factor", [P, PACK * S], F32)
        dwell = sb("dwell", [P, PACK * S], F32)
        for t in range(PACK):
            nc.scalar.activation(part(tail, t), y_bank[t][:], ACT.Sigmoid, scale=-1.0)
        for t in range(PACK):
            nc.vector.scalar_tensor_tensor(part(factor, t), y_bank[t][:], KNEE, part(slow, t), ALU.max, ALU.mult)
            nc.vector.tensor_scalar(part(floored, t), part(tail, t), math.exp(-KNEE), None, ALU.max)
        for t in range(PACK):
            nc.scalar.activation(part(log_tail, t), part(floored, t), ACT.Ln)
        for t in range(PACK):
            nc.vector.scalar_tensor_tensor(
                part(dwell, t), part(log_tail, t), -1.0 / (0.3 * KNEE), part(factor, t), ALU.mult, ALU.mult
            )

        w3_bf = sb("w3_bf", [P, PACK * N], BF16)
        w3_codes = sb("w3_codes", [P, N], U32)
        w3_scales = sb("w3_scales", [P, N], U8)
        nc.vector.tensor_copy(
            w3_bf[:].rearrange("p (c i t) -> p c t i", i=4, t=PACK),
            w3_raw[:].rearrange("p t (c i) -> p c t i", i=4),
        )
        jam_unit = sb("jam_unit", [P, PACK], F32)
        nc.vector.tensor_scalar(jam_unit[:], unit_sb[:], -0.4, None, ALU.mult)
        quantize(w3_codes, w3_scales, w3_bf, 0, N)

        def finish(hid, c0, w, j0, weave, copy_out, store, bank):
            hid_bf = sb("hid_bf%d" % j0, [P, PACK * w], BF16)
            hid_codes = sb("hid_codes%d" % j0, [P, w], U32)
            hid_scales = sb("hid_scales%d" % j0, [P, w], U8)
            result = sb("result%d" % j0, [P, w], F32)
            weave(
                hid_bf[:].rearrange("p (c i t) -> p c t i", i=4, t=PACK),
                hid[:, :, c0 : c0 + w].rearrange("p t (c i) -> p c t i", i=4),
            )
            quantize(hid_codes, hid_scales, hid_bf, 0, w)
            acc = psum.tile([P, w], F32, name="acc%d" % j0, tag="a%d" % bank)
            nc.tensor.matmul_mx(
                out=acc[:],
                lhsT=w3_codes[:].bitcast(FP8X4),
                lhsT_scale=w3_scales[:],
                rhs=hid_codes[:].bitcast(FP8X4),
                rhs_scale=hid_scales[:],
                start=True,
                stop=True,
            )
            copy_out(result[:], acc[:])
            store(out[:, j0 : j0 + w], result[:])

        for h in range(2):
            cols = slice(h * HALF, (h + 1) * HALF)
            places = nxt_sb[:, h * HALF // 16 : (h + 1) * HALF // 16]

            def pair(name):
                return [sb("%s%d%d" % (name, h, u), [P, 2, HALF], F32) for u in range(2)]

            ahead, longest, jam, root, recip, flow = [
                pair(name) for name in ("ahead", "longest", "jam", "root", "recip", "flow")
            ]
            hid = sb("hid%d" % h, [P, PACK, HALF], BF16)
            for t in range(PACK):
                window = part(dwell, t).indirect(places)
                if h == 0 and t >= 2:
                    nc.vector.tensor_copy(ahead[t // 2][:, t % 2, :], window)
                else:
                    nc.scalar.activation(ahead[t // 2][:, t % 2, :], window, ACT.Copy)
            for u in range(2):
                nc.vector.tensor_tensor(longest[u][:], ahead[u][:], cut(dwell, h, u), ALU.max)
            for u in range(2):
                nc.scalar.activation(root[u][:], longest[u][:], ACT.Abs_reciprocal_sqrt, bias=0.5)
                nc.scalar.activation(recip[u][:], root[u][:], ACT.Square)
            for u in range(2):
                nc.vector.tensor_tensor(jam[u][:], longest[u][:], cut(dwell, h, u), ALU.subtract)
            for u in range(2):
                for t in (2 * u, 2 * u + 1):
                    nc.vector.scalar_tensor_tensor(
                        flow[u][:, t % 2, :],
                        recip[u][:, t % 2, :],
                        unit_sb[:, t : t + 1],
                        part(load_sb, t)[:, cols],
                        ALU.mult,
                        ALU.mult,
                    )
                for t in (2 * u, 2 * u + 1):
                    nc.vector.scalar_tensor_tensor(
                        hid[:, t, :],
                        jam[u][:, t % 2, :],
                        jam_unit[:, t : t + 1],
                        flow[u][:, t % 2, :],
                        ALU.mult,
                        ALU.add,
                    )
            if h == 0:
                finish(hid, 0, HALF, 0, nc.scalar.copy, nc.scalar.copy, nc.sync.dma_start, 0)
            else:
                finish(hid, 0, HALF // 2, HALF, nc.vector.tensor_copy, nc.vector.tensor_copy, nc.sync.dma_start, 1)
                finish(hid, HALF // 2, HALF // 2, HALF + HALF // 2, nc.scalar.copy, nc.scalar.copy, nc.scalar.dma_start, 2)
